import numpy as np
import ml_dtypes


def mxq(x, axis, fmt="e4m3"):
    dtype, down = {"e4m3": (ml_dtypes.float8_e4m3fn, 7), "e5m2": (ml_dtypes.float8_e5m2, 14)}[fmt]
    v = np.moveaxis(np.asarray(x, np.float32).astype(ml_dtypes.bfloat16).astype(np.float64), axis, -1)
    blocks = v.reshape(v.shape[:-1] + (-1, 32))
    amax = np.abs(blocks).max(-1, keepdims=True)
    byte = np.maximum(np.where(amax > 0, np.frexp(amax)[1] - 1 + 127, 0) - down, 1)
    scale = np.exp2(byte - 127.0)
    codes = (blocks / scale).astype(np.float32).astype(dtype).astype(np.float64)
    return np.moveaxis((codes * scale).reshape(v.shape), -1, axis)


WIDE = False


def mx_kscale(k):
    if not WIDE:
        return np.ones(k)
    levels = np.array([10, -10, 5, -5, 0])
    if k % 512:
        return np.exp2(np.random.permutation(np.resize(levels, k // 32))).repeat(32)
    a = np.empty((k // 512, 16))
    for p in range(k // 512):
        a[p, :8] = np.random.permutation(np.resize(levels, 8))
        for g in range(8):
            far = levels[np.abs(levels - a[p, g]) >= 10]
            a[p, g + 8] = far[np.random.randint(len(far))]
    return np.exp2(a.ravel()).repeat(32)


def f64(x):
    return np.asarray(x).astype(np.float64)


def striped(idx):
    return np.tile(idx.reshape(-1, 16).T, (8, 1)).astype(np.uint16)


def unstriped(offs):
    return offs[:16].T.reshape(-1).astype(np.int64)


E2M1 = np.array([0.0, 0.5, 1.0, 1.5, 2.0, 3.0, 4.0, 6.0, -0.0, -0.5, -1.0, -1.5, -2.0, -3.0, -4.0, -6.0])


def pack_weight(w, fmt):
    k, n = w.shape
    w = f64(np.asarray(w, np.float32).astype(ml_dtypes.bfloat16)).reshape(k // 32, 32, n)
    amax = np.abs(w).max(1)
    if fmt == "e4m3":
        byte = np.frexp(amax)[1] - 1 + 127 - 7
    else:
        mant, ex = np.frexp(amax / 6.0)
        byte = np.where(mant > 0.5, ex, ex - 1) + 127
    byte = np.clip(np.where(amax > 0, byte, 1), 1, 254)
    scaled = (w * np.exp2(127.0 - byte)[:, None, :]).reshape(k, n).astype(np.float32)
    by_word = np.ascontiguousarray(scaled.reshape(k // 512, 128, 4, n).transpose(0, 1, 3, 2))
    if fmt == "e4m3":
        words = by_word.astype(ml_dtypes.float8_e4m3fn).view(np.uint8)
    else:
        c = by_word.astype(ml_dtypes.float4_e2m1fn).view(np.uint8) & 0xF
        words = (c[..., 0::2] | (c[..., 1::2] << 4)).reshape(k // 512, 128, 2 * n)
    return np.ascontiguousarray(words), np.ascontiguousarray(byte.astype(np.uint8).reshape(k // 512, 16, n))


def unpack_weight(words, scales, fmt):
    g, _, n = scales.shape
    words = np.ascontiguousarray(words).reshape(g, 128, n, -1)
    if fmt == "e4m3":
        vals = words.view(ml_dtypes.float8_e4m3fn).astype(np.float64)
    else:
        nib = np.empty((g, 128, n, 4), np.uint8)
        nib[..., 0::2] = words & 0xF
        nib[..., 1::2] = words >> 4
        vals = E2M1[nib]
    vals = vals * np.repeat(np.exp2(scales.astype(np.float64) - 127.0), 8, axis=1)[..., None]
    return vals.transpose(0, 1, 3, 2).reshape(g * 512, n)


def gelu(v):
    return 0.5 * v * (1.0 + np.tanh(np.sqrt(2.0 / np.pi) * (v + 0.044715 * v**3)))


K, T, S, P, T2, M, H, N = 1024, 4096, 1024, 1024, 2048, 512, 1024, 384


def setup_inputs():
    n = np.random.standard_normal
    s, u1, u = mx_kscale(K)[:, None], mx_kscale(M)[:, None], mx_kscale(H)[:, None]
    d = {}
    d["tab_words"], d["tab_scales"] = pack_weight(n((K, T)) * s, "e4m3")
    d["offs"] = striped(np.random.permutation(T)[:S])
    d["offs2"] = striped(np.random.permutation(T2)[:S])
    d["offs3"] = striped(np.random.permutation(T2)[:P])
    d["offs4"] = striped(np.random.permutation(T2)[:P])
    d["w1"] = (1.6 * n((K, M)) / s / K**0.5).astype(np.float32)
    d["w2_words"], d["w2_scales"] = pack_weight(n((K, M)) / s / K**0.5, "e2m1")
    d["lift"] = (np.exp(0.3 * n(M)) * u1[:, 0]).astype(np.float32)
    d["w3"] = (n((M, H)) / u1 * u.T / M**0.5).astype(np.float32)
    d["wgs"] = np.exp(0.3 * n((128, S))).astype(np.float32)
    d["page0"] = (n((H, T2)) * u).astype(np.float32)
    d["gain"] = np.exp(0.4 * n(H)).astype(np.float32)
    d["w4_words"], d["w4_scales"] = pack_weight(0.8 * n((H, N)) / u / H**0.5, "e4m3")
    d["cap"] = (0.3 + 0.6 * n(N)).astype(np.float32)
    d["wgo"] = np.exp(0.3 * n((128, P))).astype(np.float32)
    d["page1"] = n((N, T2)).astype(np.float32)
    return d


def reference(tab_words, tab_scales, offs, offs2, offs3, offs4, w1, w2_words, w2_scales, lift, w3, wgs, page0, gain, w4_words, w4_scales, cap, wgo, page1):
    v = unpack_weight(tab_words, tab_scales, "e4m3")[:, unstriped(offs)]
    a = mxq(f64(w1), 0, "e4m3").T @ v
    b = unpack_weight(w2_words, w2_scales, "e2m1").T @ v
    top = np.maximum(a / (1.0 + np.exp(-a)), b) * f64(lift)[:, None]
    h = mxq(f64(w3), 0, "e4m3").T @ mxq(top, 0, "e4m3")
    page = f64(page0).copy()
    page[:, unstriped(offs2)] = np.tile(f64(wgs), (H // 128, 1)) * h
    x = page[:, unstriped(offs3)] * f64(gain)[:, None]
    y = unpack_weight(w4_words, w4_scales, "e4m3").T @ mxq(x, 0, "e4m3")
    y = np.minimum(y, f64(cap)[:, None])
    out = f64(page1).copy()
    out[:, unstriped(offs4)] = np.tile(f64(wgo), (N // 128, 1)) * y
    return out

@@ -1,0 +1,325 @@
+from contextlib import ExitStack
+
+import concourse.mybir as mybir
+
+K, T, S, PICKS, T2, M, H, N = 1024, 4096, 1024, 1024, 2048, 512, 1024, 384
+FLOPS = 2 * (2 * K * M * S + M * H * S + H * N * PICKS)
+
+F32 = mybir.dt.float32
+BF16 = mybir.dt.bfloat16
+I32 = mybir.dt.int32
+U32 = mybir.dt.uint32
+U16 = mybir.dt.uint16
+U8 = mybir.dt.uint8
+FP8X4 = mybir.dt.float8_e4m3fn_x4
+FP4X4 = mybir.dt.float4_e2m1fn_x4
+ALU = mybir.AluOpType
+ACT = mybir.ActivationFunctionType
+
+P = 128
+C = 512
+LC = C // 16
+
+
+def tile_list_call_triage_page_kernel(
+    tc, tab_words, tab_scales, offs, offs2, offs3, offs4, w1, w2_words, w2_scales, lift, w3, wgs, page0, gain,
+    w4_words, w4_scales, cap, wgo, page1, out,
+):
+    nc = tc.nc
+    with ExitStack() as ctx:
+        sb = ctx.enter_context(tc.tile_pool(name="sb", bufs=1))
+        ps = ctx.enter_context(tc.psum_pool(name="ps", bufs=1))
+
+        def tile(name, shape, dtype, tag=None):
+            return sb.tile(shape, dtype, name=name, tag=tag or name, align_bytes=64)
+
+        banks = [ps.tile([P, C], F32, name="bank%d" % i) for i in range(8)]
+
+        lists = [tile("list%d" % i, [P, 64], U16) for i in range(4)]
+        o1, o2, o3, o4 = lists
+        tsc = tile("tsc", [P, T], U8)
+        gs = tile("gs", [P, S], U8)
+        vs = [tile("vs%d" % a, [P, S], U8) for a in range(2)]
+        tabw = [tile("tabw%d" % a, [P, T], U32, tag="slab%d" % a) for a in range(2)]
+        vw = [[tile("vw%d%d" % (a, c), [P, C], U32) for c in range(2)] for a in range(2)]
+        w2r = tile("w2r", [P, 2, 2 * M], U8)
+        w2d = [tile("w2d%d" % a, [P, 2 * M], U8) for a in range(2)]
+        w2sr = tile("w2sr", [P, 2, M], U8)
+        w2s = [tile("w2s%d" % a, [P, M], U8) for a in range(2)]
+        w1c = [tile("w1c%d" % a, [P, M], U32) for a in range(2)]
+        w1s = [tile("w1s%d" % a, [P, M], U8) for a in range(2)]
+        w3c = [tile("w3c%d" % a, [P, 512], U32) for a in range(2)]
+        w3s = [tile("w3s%d" % a, [P, 512], U8) for a in range(2)]
+        w4c = tile("w4c", [P, 2, N], U32)
+        w4s = tile("w4s", [P, 2, N], U8)
+        lift_sb = tile("lift_sb", [P, 4], F32)
+        gain_sb = tile("gain_sb", [P, 2, 4], F32)
+        cap_sb = tile("cap_sb", [P, 3], F32)
+        wd = [tile("wd%d" % t, [P, S], F32) for t in range(4)]
+        wgo_sb = tile("wgo_sb", [P, PICKS], F32)
+        sm = [tile("sm%d" % c, [P, 4, C], F32) for c in range(2)]
+        planes = [tile("planes%d" % i, [P, 4, C], BF16) for i in range(3)]
+        inter = [tile("inter%d" % i, [P, 4 * C], BF16) for i in range(3)]
+        tcode = [tile("tcode%d" % c, [P, C], U32) for c in range(2)]
+        tscale = [tile("tscale%d" % c, [P, C], U8) for c in range(2)]
+        hs = [tile("hs%d" % i, [P, S], F32) for i in range(2)]
+        xs = [tile("xs%d" % i, [P, PICKS], F32) for i in range(2)]
+        xc = [[tile("xc%d%d" % (a, c), [P, C], U32) for c in range(2)] for a in range(2)]
+        xsc = [[tile("xsc%d%d" % (a, c), [P, C], U8) for c in range(2)] for a in range(2)]
+
+        nc.vector.memset(tsc[32:64, :].bitcast(I32), 0)
+        nc.vector.memset(tsc[64:128, :].bitcast(I32), 0)
+        nc.vector.memset(w2sr[:].rearrange("p a m -> p (a m)").bitcast(I32), 0)
+        for a in range(2):
+            nc.vector.memset(vs[a][:].bitcast(I32), 0)
+        nc.vector.memset(w4s[:].rearrange("p a m -> p (a m)").bitcast(I32), 0)
+
+        def load_scale_rows(dst, src):
+            for q in range(4):
+                nc.sync.dma_start(
+                    out=dst[32 * q : 32 * q + 4].bitcast(I32),
+                    in_=src[:, 4 * q : 4 * q + 4, :].rearrange("a r n -> r a n").bitcast(I32),
+                )
+
+        def load_raw(name, slot, rows):
+            raw = tile(name, [P, 4, 512], F32, tag="raw%d" % slot)
+            nc.sync.dma_start(out=raw[:], in_=rows.rearrange("(p j) c -> p j c", j=4))
+            return raw
+
+        def load_tab(a):
+            nc.sync.dma_start(
+                out=tabw[a][:].bitcast(I32), in_=tab_words[a].rearrange("p t i -> p (t i)").bitcast(I32)
+            )
+
+        pages = {}
+
+        def load_page(a, t):
+            i = 4 * a + t
+            pages[a, t] = tile("page%d" % i, [P, T2], F32, tag="page%d" % (i % 7))
+            nc.sync.dma_start(out=pages[a, t][:], in_=page0.rearrange("(a p t) c -> a t p c", a=2, t=4)[a, t])
+
+        def load_wd(t):
+            rows = wgs.rearrange("(i t) j -> t i j", t=4)[t]
+            for g in range(4):
+                nc.sync.dma_start(out=wd[t][32 * g : 32 * g + 32, :], in_=rows)
+
+        nc.sync.dma_start(o1[:], offs)
+        nc.sync.dma_start(out=tsc[0:32, :].bitcast(I32), in_=tab_scales.rearrange("a q t -> (a q) t").bitcast(I32))
+        nc.sync.dma_start(out=w2r[:].bitcast(I32), in_=w2_words.rearrange("a p w -> p a w").bitcast(I32))
+        load_tab(0)
+        load_scale_rows(w2sr, w2_scales)
+        w1r = [load_raw("w1r%d" % a, a, w1[512 * a : 512 * a + 512, :]) for a in range(2)]
+        load_tab(1)
+        nc.sync.dma_start(out=lift_sb[:], in_=lift.rearrange("(p t) -> p t", t=4))
+
+        nc.vector.tensor_copy(gs[:], tsc[:].indirect(o1[:]))
+        for a in range(2):
+            for q in range(4):
+                nc.gpsimd.dma_start(
+                    out=vs[a][32 * q : 32 * q + 4, :].bitcast(I32),
+                    in_=gs[16 * a + 4 * q : 16 * a + 4 * q + 4, :].bitcast(I32),
+                )
+        for a in range(2):
+            nc.vector.tensor_copy(
+                w2d[a][:].rearrange("p (t q b) -> p q t b", t=4, b=2),
+                w2r[:, a, :].rearrange("p (q t b) -> p q t b", t=4, b=2),
+            )
+            nc.vector.tensor_copy(
+                w2s[a][:].rearrange("p (t q) -> p q t", t=4), w2sr[:, a, :].rearrange("p (q t) -> p q t", t=4)
+            )
+
+        def gather_words(a, c):
+            nc.vector.tensor_copy(vw[a][c][:], tabw[a][:].indirect(o1[:, LC * c : LC * c + LC]))
+
+        def cast_weight(raw, dst):
+            nc.scalar.copy(
+                dst[:].rearrange("p (t q j) -> p q j t", t=4, j=4), raw[:].rearrange("p j (q t) -> p q j t", t=4)
+            )
+
+        def quantize(src, codes, scales):
+            nc.vector.quantize_mx(out=codes[:].bitcast(FP8X4), scales=scales[:], in_=src[:])
+
+        def interleave(copy, src, dst):
+            copy(
+                dst[:].rearrange("p (c i t) -> p c t i", i=4, t=4), src[:].rearrange("p t (c i) -> p c t i", i=4)
+            )
+
+        gather_words(0, 0)
+        gather_words(0, 1)
+        for a in range(2):
+            cast_weight(w1r[a], inter[a])
+            quantize(inter[a], w1c[a], w1s[a])
+
+        w3r0 = load_raw("w3r0", 0, w3[:, 0:512])
+        load_wd(0)
+        load_page(0, 0)
+        nc.sync.dma_start(o2[:], offs2)
+        load_wd(1)
+        load_page(0, 1)
+        load_wd(2)
+        load_page(0, 2)
+        nc.sync.dma_start(o3[:], offs3)
+        nc.sync.dma_start(out=gain_sb[:], in_=gain.rearrange("(a p t) -> p a t", a=2, t=4))
+        load_wd(3)
+        load_page(0, 3)
+        w3r1 = load_raw("w3r1", 1, w3[:, 512:1024])
+        for t in range(3):
+            load_page(1, t)
+        nc.sync.dma_start(
+            out=w4c[:].bitcast(I32), in_=w4_words.rearrange("a p c i -> p a (c i)").bitcast(I32)
+        )
+        load_scale_rows(w4s, w4_scales)
+        nc.sync.dma_start(o4[:], offs4)
+        nc.sync.dma_start(out=wgo_sb[:], in_=wgo)
+        with nc.allow_non_contiguous_dma(reason="one cap value for each partition and row tile"):
+            nc.sync.dma_start(out=cap_sb[:], in_=cap.rearrange("(c p) -> p c", p=P))
+
+        def stage1_pass(a, c, t):
+            cols = slice(128 * t, 128 * t + 128)
+            nc.tensor.matmul_mx(
+                out=banks[2 * t][:], lhsT=w1c[a][:, cols].bitcast(FP8X4), lhsT_scale=w1s[a][:, cols],
+                rhs=vw[a][c][:].bitcast(FP8X4), rhs_scale=vs[a][:, C * c : C * c + C], start=a == 0, stop=a == 1,
+            )
+            nc.tensor.matmul_mx(
+                out=banks[2 * t + 1][:], lhsT=w2d[a][:, 256 * t : 256 * t + 256].bitcast(FP4X4),
+                lhsT_scale=w2s[a][:, cols],
+                rhs=vw[a][c][:].bitcast(FP8X4), rhs_scale=vs[a][:, C * c : C * c + C], start=a == 0, stop=a == 1,
+            )
+
+        def silu(c, t):
+            nc.scalar.activation(sm[c][:, t, :], banks[2 * t][:], ACT.Silu)
+
+        def larger(c, t):
+            nc.vector.tensor_tensor(sm[c][:, t, :], banks[2 * t + 1][:], sm[c][:, t, :], ALU.max)
+
+        def lifted(c, t):
+            nc.scalar.activation(planes[c][:, t, :], sm[c][:, t, :], ACT.Copy, scale=lift_sb[:, t : t + 1])
+
+        for t in range(4):
+            stage1_pass(0, 0, t)
+        gather_words(1, 0)
+        gather_words(1, 1)
+        for t in range(4):
+            stage1_pass(1, 0, t)
+        for t in range(4):
+            silu(0, t)
+            larger(0, t)
+            if t:
+                lifted(0, t - 1)
+            stage1_pass(0, 1, t)
+            stage1_pass(1, 1, t)
+        lifted(0, 3)
+        cast_weight(w3r0, inter[2])
+        interleave(nc.vector.tensor_copy, planes[0], inter[0])
+        quantize(inter[2], w3c[0], w3s[0])
+        quantize(inter[0], tcode[0], tscale[0])
+        for t in range(4):
+            silu(1, t)
+            larger(1, t)
+
+        turn = [0]
+
+        def put(a, t, chunks):
+            stage = hs[turn[0] % 2]
+            for c in chunks:
+                bank = banks[turn[0] % 2 * 2 + c]
+                nc.tensor.matmul_mx(
+                    out=bank[:], lhsT=w3c[a][:, 128 * t : 128 * t + 128].bitcast(FP8X4),
+                    lhsT_scale=w3s[a][:, 128 * t : 128 * t + 128],
+                    rhs=tcode[c][:].bitcast(FP8X4), rhs_scale=tscale[c][:], start=True, stop=True,
+                )
+                nc.scalar.copy(stage[:, C * c : C * c + C], bank[:])
+            lo, hi = chunks[0], chunks[-1] + 1
+            nc.vector.tensor_tensor(
+                pages[a, t][:].indirect(o2[:, LC * lo : LC * hi]), stage[:, C * lo : C * hi], wd[t][:, C * lo : C * hi],
+                ALU.mult,
+            )
+            turn.append(turn.pop() + 1)
+
+        def fetch(a, t, chunks, dst, x_planes):
+            lo, hi = chunks[0], chunks[-1] + 1
+            nc.vector.tensor_copy(dst, pages[a, t][:].indirect(o3[:, LC * lo : LC * hi]))
+            for c in chunks:
+                nc.scalar.activation(
+                    x_planes[c][:, t, :], dst[:, C * (c - lo) : C * (c - lo + 1)], ACT.Copy,
+                    scale=gain_sb[:, a, t : t + 1],
+                )
+
+        put(0, 0, [0])
+        for t in range(4):
+            lifted(1, t)
+        put(0, 1, [0])
+        interleave(nc.scalar.copy, planes[1], inter[1])
+        quantize(inter[1], tcode[1], tscale[1])
+        put(0, 2, [0])
+        put(0, 0, [1])
+        put(0, 1, [1])
+        xp0 = [planes[2], planes[0]]
+        xp1 = [planes[1], planes[2]]
+        fetch(0, 0, [0, 1], xs[0][:], xp0)
+        load_page(1, 3)
+        outs = [
+            tile("out0", [P, T2], F32, tag="slab0"),
+            tile("out1", [P, T2], F32, tag="slab1"),
+            tile("out2", [P, T2], F32, tag="raw0"),
+        ]
+        for n in range(3):
+            nc.sync.dma_start(out=outs[n][:], in_=page1[P * n : P * n + P, :])
+        put(0, 2, [1])
+        fetch(0, 1, [0, 1], xs[1][:], xp0)
+        cast_weight(w3r1, inter[2])
+        put(0, 3, [0, 1])
+        quantize(inter[2], w3c[1], w3s[1])
+        fetch(0, 2, [0, 1], xs[0][:], xp0)
+        put(1, 0, [0, 1])
+        fetch(0, 3, [0, 1], xs[1][:], xp0)
+        put(1, 1, [0, 1])
+        halves = [xs[i // 2][:, C * (i % 2) : C * (i % 2) + C] for i in range(4)]
+        for c in range(2):
+            interleave(nc.scalar.copy, xp0[c], inter[c])
+        fetch(1, 0, [0], halves[0], xp1)
+        put(1, 2, [0, 1])
+        for c in range(2):
+            quantize(inter[c], xc[0][c], xsc[0][c])
+        fetch(1, 1, [0], halves[1], xp1)
+        put(1, 3, [0, 1])
+        fetch(1, 2, [0], halves[2], xp1)
+        fetch(1, 3, [0], halves[3], xp1)
+        interleave(nc.scalar.copy, xp1[0], inter[2])
+        for t, h in ((2, 0), (0, 2), (1, 3), (3, 1)):
+            fetch(1, t, [1], halves[h], xp1)
+
+        def scores(c):
+            quantize(inter[2 - 2 * c], xc[1][c], xsc[1][c])
+            for n in range(3):
+                bank = banks[4 + n if c == 0 else n]
+                cols = slice(P * n, P * n + P)
+                for a in range(2):
+                    nc.tensor.matmul_mx(
+                        out=bank[:], lhsT=w4c[:, a, cols].bitcast(FP8X4), lhsT_scale=w4s[:, a, cols],
+                        rhs=xc[a][c][:].bitcast(FP8X4), rhs_scale=xsc[a][c][:], start=a == 0, stop=a == 1,
+                    )
+
+        def capped(c, n):
+            nc.vector.scalar_tensor_tensor(
+                sm[c][:, n, :], banks[4 + n if c == 0 else n][:], cap_sb[:, n : n + 1], wgo_sb[:, C * c : C * c + C],
+                ALU.min, ALU.mult,
+            )
+
+        def place(c, n):
+            nc.vector.tensor_copy(outs[n][:].indirect(o4[:, LC * c : LC * c + LC]), sm[c][:, n, :])
+
+        scores(0)
+        interleave(nc.scalar.copy, xp1[1], inter[0])
+        capped(0, 0)
+        capped(0, 1)
+        place(0, 0)
+        capped(0, 2)
+        place(0, 1)
+        scores(1)
+        place(0, 2)
+        for n in range(3):
+            capped(1, n)
+        for n in range(3):
+            place(1, n)
+            nc.sync.dma_start(out=out[P * n : P * n + P, :], in_=outs[n][:])

@@ -39,7 +39,7 @@ def tile_list_call_triage_page_kernel(
         o1, o2, o3, o4 = lists
         tsc = tile("tsc", [P, T], U8)
         gs = tile("gs", [P, S], U8)
-        vs = [tile("vs%d" % a, [P, S], U8) for a in range(2)]
+        vs = [tile("vs0", [P, S], U8)]
         tabw = [tile("tabw%d" % a, [P, T], U32, tag="slab%d" % a) for a in range(2)]
         vw = [[tile("vw%d%d" % (a, c), [P, C], U32) for c in range(2)] for a in range(2)]
         w2r = tile("w2r", [P, 2, 2 * M], U8)
@@ -56,7 +56,6 @@ def tile_list_call_triage_page_kernel(
         gain_sb = tile("gain_sb", [P, 2, 4], F32)
         cap_sb = tile("cap_sb", [P, 3], F32)
         wd = [tile("wd%d" % t, [P, S], F32) for t in range(4)]
-        wgo_sb = tile("wgo_sb", [P, PICKS], F32)
         sm = [tile("sm%d" % c, [P, 4, C], F32) for c in range(2)]
         planes = [tile("planes%d" % i, [P, 4, C], BF16) for i in range(3)]
         inter = [tile("inter%d" % i, [P, 4 * C], BF16) for i in range(3)]
@@ -64,14 +63,13 @@ def tile_list_call_triage_page_kernel(
         tscale = [tile("tscale%d" % c, [P, C], U8) for c in range(2)]
         hs = [tile("hs%d" % i, [P, S], F32) for i in range(2)]
         xs = [tile("xs%d" % i, [P, PICKS], F32) for i in range(2)]
-        xc = [[tile("xc%d%d" % (a, c), [P, C], U32) for c in range(2)] for a in range(2)]
+        xc = {(1, c): tile("xc1%d" % c, [P, C], U32) for c in range(2)}
         xsc = [[tile("xsc%d%d" % (a, c), [P, C], U8) for c in range(2)] for a in range(2)]
 
+        nc.vector.memset(w2sr[:].rearrange("p a m -> p (a m)").bitcast(I32), 0)
         nc.vector.memset(tsc[32:64, :].bitcast(I32), 0)
         nc.vector.memset(tsc[64:128, :].bitcast(I32), 0)
-        nc.vector.memset(w2sr[:].rearrange("p a m -> p (a m)").bitcast(I32), 0)
-        for a in range(2):
-            nc.vector.memset(vs[a][:].bitcast(I32), 0)
+        nc.vector.memset(vs[0][:].bitcast(I32), 0)
         nc.vector.memset(w4s[:].rearrange("p a m -> p (a m)").bitcast(I32), 0)
 
         def load_scale_rows(dst, src):
@@ -106,19 +104,22 @@ def tile_list_call_triage_page_kernel(
         nc.sync.dma_start(o1[:], offs)
         nc.sync.dma_start(out=tsc[0:32, :].bitcast(I32), in_=tab_scales.rearrange("a q t -> (a q) t").bitcast(I32))
         nc.sync.dma_start(out=w2r[:].bitcast(I32), in_=w2_words.rearrange("a p w -> p a w").bitcast(I32))
-        load_tab(0)
         load_scale_rows(w2sr, w2_scales)
+        load_tab(0)
         w1r = [load_raw("w1r%d" % a, a, w1[512 * a : 512 * a + 512, :]) for a in range(2)]
         load_tab(1)
         nc.sync.dma_start(out=lift_sb[:], in_=lift.rearrange("(p t) -> p t", t=4))
 
         nc.vector.tensor_copy(gs[:], tsc[:].indirect(o1[:]))
-        for a in range(2):
+
+        def move_scale_rows(a):
             for q in range(4):
-                nc.gpsimd.dma_start(
+                nc.scalar.dma_start(
                     out=vs[a][32 * q : 32 * q + 4, :].bitcast(I32),
                     in_=gs[16 * a + 4 * q : 16 * a + 4 * q + 4, :].bitcast(I32),
                 )
+
+        move_scale_rows(0)
         for a in range(2):
             nc.vector.tensor_copy(
                 w2d[a][:].rearrange("p (t q b) -> p q t b", t=4, b=2),
@@ -131,9 +132,10 @@ def tile_list_call_triage_page_kernel(
         def gather_words(a, c):
             nc.vector.tensor_copy(vw[a][c][:], tabw[a][:].indirect(o1[:, LC * c : LC * c + LC]))
 
-        def cast_weight(raw, dst):
-            nc.scalar.copy(
-                dst[:].rearrange("p (t q j) -> p q j t", t=4, j=4), raw[:].rearrange("p j (q t) -> p q j t", t=4)
+        def cast_weight(raw, dst, copy=nc.scalar.copy, q=slice(0, 128)):
+            copy(
+                dst[:].rearrange("p (t q j) -> p q j t", t=4, j=4)[:, q],
+                raw[:].rearrange("p j (q t) -> p q j t", t=4)[:, q],
             )
 
         def quantize(src, codes, scales):
@@ -146,23 +148,27 @@ def tile_list_call_triage_page_kernel(
 
         gather_words(0, 0)
         gather_words(0, 1)
-        for a in range(2):
-            cast_weight(w1r[a], inter[a])
-            quantize(inter[a], w1c[a], w1s[a])
+        cast_weight(w1r[0], inter[0])
+        vs.append(tile("vs1", [P, S], U8, tag="raw0"))
+        nc.vector.memset(vs[1][:].bitcast(I32), 0)
+        move_scale_rows(1)
+        quantize(inter[0], w1c[0], w1s[0])
+        cast_weight(w1r[1], inter[1])
+        quantize(inter[1], w1c[1], w1s[1])
 
-        w3r0 = load_raw("w3r0", 0, w3[:, 0:512])
+        w3r0 = load_raw("w3r0", 2, w3[:, 0:512])
         load_wd(0)
         load_page(0, 0)
         nc.sync.dma_start(o2[:], offs2)
         load_wd(1)
         load_page(0, 1)
+        w3r1 = load_raw("w3r1", 1, w3[:, 512:1024])
         load_wd(2)
         load_page(0, 2)
         nc.sync.dma_start(o3[:], offs3)
         nc.sync.dma_start(out=gain_sb[:], in_=gain.rearrange("(a p t) -> p a t", a=2, t=4))
         load_wd(3)
         load_page(0, 3)
-        w3r1 = load_raw("w3r1", 1, w3[:, 512:1024])
         for t in range(3):
             load_page(1, t)
         nc.sync.dma_start(
@@ -170,6 +176,7 @@ def tile_list_call_triage_page_kernel(
         )
         load_scale_rows(w4s, w4_scales)
         nc.sync.dma_start(o4[:], offs4)
+        wgo_sb = tile("wgo_sb", [P, PICKS], F32, tag="tsc")
         nc.sync.dma_start(out=wgo_sb[:], in_=wgo)
         with nc.allow_non_contiguous_dma(reason="one cap value for each partition and row tile"):
             nc.sync.dma_start(out=cap_sb[:], in_=cap.rearrange("(c p) -> p c", p=P))
@@ -206,35 +213,40 @@ def tile_list_call_triage_page_kernel(
             larger(0, t)
             if t:
                 lifted(0, t - 1)
+            cast_weight(w3r0, inter[2], nc.vector.tensor_copy, slice(32 * t, 32 * t + 32))
             stage1_pass(0, 1, t)
             stage1_pass(1, 1, t)
         lifted(0, 3)
-        cast_weight(w3r0, inter[2])
-        interleave(nc.vector.tensor_copy, planes[0], inter[0])
         quantize(inter[2], w3c[0], w3s[0])
+        interleave(nc.vector.tensor_copy, planes[0], inter[0])
         quantize(inter[0], tcode[0], tscale[0])
         for t in range(4):
             silu(1, t)
-            larger(1, t)
 
-        turn = [0]
+        steps = [(0, 0, [0]), (0, 1, [0]), (0, 2, [0]), (0, 0, [1]), (0, 1, [1]), (0, 2, [1]), (0, 3, [0, 1])]
+        steps.extend((1, t, [0, 1]) for t in range(4))
 
-        def put(a, t, chunks):
-            stage = hs[turn[0] % 2]
+        stages = [hs[i % 2][:] for i in range(len(steps))]
+        stages[2] = planes[1][:].rearrange("p t c -> p (t c)").bitcast(F32)
+
+        def states(i):
+            a, t, chunks = steps[i]
             for c in chunks:
-                bank = banks[turn[0] % 2 * 2 + c]
+                bank = banks[i % 2 * 2 + c]
                 nc.tensor.matmul_mx(
                     out=bank[:], lhsT=w3c[a][:, 128 * t : 128 * t + 128].bitcast(FP8X4),
                     lhsT_scale=w3s[a][:, 128 * t : 128 * t + 128],
                     rhs=tcode[c][:].bitcast(FP8X4), rhs_scale=tscale[c][:], start=True, stop=True,
                 )
-                nc.scalar.copy(stage[:, C * c : C * c + C], bank[:])
+                nc.scalar.copy(stages[i][:, C * c : C * c + C], bank[:])
+
+        def put(i):
+            a, t, chunks = steps[i]
             lo, hi = chunks[0], chunks[-1] + 1
             nc.vector.tensor_tensor(
-                pages[a, t][:].indirect(o2[:, LC * lo : LC * hi]), stage[:, C * lo : C * hi], wd[t][:, C * lo : C * hi],
-                ALU.mult,
+                pages[a, t][:].indirect(o2[:, LC * lo : LC * hi]), stages[i][:, C * lo : C * hi],
+                wd[t][:, C * lo : C * hi], ALU.mult,
             )
-            turn.append(turn.pop() + 1)
 
         def fetch(a, t, chunks, dst, x_planes):
             lo, hi = chunks[0], chunks[-1] + 1
@@ -245,15 +257,25 @@ def tile_list_call_triage_page_kernel(
                     scale=gain_sb[:, a, t : t + 1],
                 )
 
-        put(0, 0, [0])
+        states(0)
+        states(1)
+        put(0)
         for t in range(4):
+            larger(1, t)
             lifted(1, t)
-        put(0, 1, [0])
+        put(1)
         interleave(nc.scalar.copy, planes[1], inter[1])
+        states(2)
         quantize(inter[1], tcode[1], tscale[1])
-        put(0, 2, [0])
-        put(0, 0, [1])
-        put(0, 1, [1])
+        cast_weight(w3r1, inter[2])
+        states(3)
+        put(2)
+        quantize(inter[2], w3c[1], w3s[1])
+        states(4)
+        put(3)
+        states(5)
+        put(4)
+        states(6)
         xp0 = [planes[2], planes[0]]
         xp1 = [planes[1], planes[2]]
         fetch(0, 0, [0, 1], xs[0][:], xp0)
@@ -261,65 +283,73 @@ def tile_list_call_triage_page_kernel(
         outs = [
             tile("out0", [P, T2], F32, tag="slab0"),
             tile("out1", [P, T2], F32, tag="slab1"),
-            tile("out2", [P, T2], F32, tag="raw0"),
+            tile("out2", [P, T2], F32, tag="raw2"),
         ]
         for n in range(3):
             nc.sync.dma_start(out=outs[n][:], in_=page1[P * n : P * n + P, :])
-        put(0, 2, [1])
+        put(5)
+        states(7)
         fetch(0, 1, [0, 1], xs[1][:], xp0)
-        cast_weight(w3r1, inter[2])
-        put(0, 3, [0, 1])
-        quantize(inter[2], w3c[1], w3s[1])
+        put(6)
+        states(8)
         fetch(0, 2, [0, 1], xs[0][:], xp0)
-        put(1, 0, [0, 1])
+        put(7)
+        states(9)
         fetch(0, 3, [0, 1], xs[1][:], xp0)
-        put(1, 1, [0, 1])
+        put(8)
+        states(10)
         halves = [xs[i // 2][:, C * (i % 2) : C * (i % 2) + C] for i in range(4)]
-        for c in range(2):
-            interleave(nc.scalar.copy, xp0[c], inter[c])
         fetch(1, 0, [0], halves[0], xp1)
-        put(1, 2, [0, 1])
-        for c in range(2):
-            quantize(inter[c], xc[0][c], xsc[0][c])
+        interleave(nc.scalar.copy, xp0[0], inter[0])
+        xc[0, 0] = tile("xc00", [P, C], U32, tag="wd1")
+        quantize(inter[0], xc[0, 0], xsc[0][0])
+        put(9)
         fetch(1, 1, [0], halves[1], xp1)
-        put(1, 3, [0, 1])
+        interleave(nc.scalar.copy, xp0[1], inter[1])
+        xc[0, 1] = tile("xc01", [P, C], U32, tag="wd2")
+        quantize(inter[1], xc[0, 1], xsc[0][1])
+        put(10)
         fetch(1, 2, [0], halves[2], xp1)
         fetch(1, 3, [0], halves[3], xp1)
         interleave(nc.scalar.copy, xp1[0], inter[2])
-        for t, h in ((2, 0), (0, 2), (1, 3), (3, 1)):
-            fetch(1, t, [1], halves[h], xp1)
+        fetch(1, 3, [1], halves[0], xp1)
+        fetch(1, 2, [1], hs[0][:, 0:C], xp1)
+        fetch(1, 0, [1], hs[0][:, C : 2 * C], xp1)
 
         def scores(c):
-            quantize(inter[2 - 2 * c], xc[1][c], xsc[1][c])
+            quantize(inter[2 - 2 * c], xc[1, c], xsc[1][c])
             for n in range(3):
                 bank = banks[4 + n if c == 0 else n]
                 cols = slice(P * n, P * n + P)
                 for a in range(2):
                     nc.tensor.matmul_mx(
                         out=bank[:], lhsT=w4c[:, a, cols].bitcast(FP8X4), lhsT_scale=w4s[:, a, cols],
-                        rhs=xc[a][c][:].bitcast(FP8X4), rhs_scale=xsc[a][c][:], start=a == 0, stop=a == 1,
+                        rhs=xc[a, c][:].bitcast(FP8X4), rhs_scale=xsc[a][c][:], start=a == 0, stop=a == 1,
                     )
 
-        def capped(c, n):
+        def capped(c, n, dst):
             nc.vector.scalar_tensor_tensor(
-                sm[c][:, n, :], banks[4 + n if c == 0 else n][:], cap_sb[:, n : n + 1], wgo_sb[:, C * c : C * c + C],
+                dst, banks[4 + n if c == 0 else n][:], cap_sb[:, n : n + 1], wgo_sb[:, C * c : C * c + C],
                 ALU.min, ALU.mult,
             )
 
-        def place(c, n):
-            nc.vector.tensor_copy(outs[n][:].indirect(o4[:, LC * c : LC * c + LC]), sm[c][:, n, :])
+        def place(c, n, src):
+            nc.vector.tensor_copy(outs[n][:].indirect(o4[:, LC * c : LC * c + LC]), src)
 
         scores(0)
+        last_x = tile("last_x", [P, C], F32, tag="inter2")
+        fetch(1, 1, [1], last_x[:], xp1)
         interleave(nc.scalar.copy, xp1[1], inter[0])
-        capped(0, 0)
-        capped(0, 1)
-        place(0, 0)
-        capped(0, 2)
-        place(0, 1)
+        capped(0, 0, sm[0][:, 0, :])
+        capped(0, 1, sm[0][:, 1, :])
+        place(0, 0, sm[0][:, 0, :])
+        place(0, 1, sm[0][:, 1, :])
         scores(1)
-        place(0, 2)
+        late_y = tile("late_y", [P, C], F32, tag="inter0")
+        capped(0, 2, late_y[:])
+        place(0, 2, late_y[:])
         for n in range(3):
-            capped(1, n)
+            capped(1, n, sm[1][:, n, :])
         for n in range(3):
-            place(1, n)
+            place(1, n, sm[1][:, n, :])
             nc.sync.dma_start(out=out[P * n : P * n + P, :], in_=outs[n][:])

@@ -17,8 +17,10 @@ ALU = mybir.AluOpType
 ACT = mybir.ActivationFunctionType
 
 P = 128
+PASS = 512
 C = 512
 LC = C // 16
+N_TILES = N // P
 
 
 def tile_list_call_triage_page_kernel(
@@ -35,227 +37,213 @@ def tile_list_call_triage_page_kernel(
 
         banks = [ps.tile([P, C], F32, name="bank%d" % i) for i in range(8)]
 
-        lists = [tile("list%d" % i, [P, 64], U16) for i in range(4)]
-        o1, o2, o3, o4 = lists
-        tsc = tile("tsc", [P, T], U8)
-        gs = tile("gs", [P, S], U8)
-        vs = [tile("vs0", [P, S], U8)]
-        tabw = [tile("tabw%d" % a, [P, T], U32, tag="slab%d" % a) for a in range(2)]
-        vw = [[tile("vw%d%d" % (a, c), [P, C], U32) for c in range(2)] for a in range(2)]
-        w2r = tile("w2r", [P, 2, 2 * M], U8)
-        w2d = [tile("w2d%d" % a, [P, 2 * M], U8) for a in range(2)]
-        w2sr = tile("w2sr", [P, 2, M], U8)
-        w2s = [tile("w2s%d" % a, [P, M], U8) for a in range(2)]
-        w1c = [tile("w1c%d" % a, [P, M], U32) for a in range(2)]
-        w1s = [tile("w1s%d" % a, [P, M], U8) for a in range(2)]
-        w3c = [tile("w3c%d" % a, [P, 512], U32) for a in range(2)]
-        w3s = [tile("w3s%d" % a, [P, 512], U8) for a in range(2)]
-        w4c = tile("w4c", [P, 2, N], U32)
-        w4s = tile("w4s", [P, 2, N], U8)
+        idx, idx2, idx3, idx4 = [tile("list%d" % i, [P, S // 16], U16) for i in range(4)]
+        tab_sc = tile("tab_sc", [P, T], U8)
+        picked_sc = tile("picked_sc", [P, S], U8)
+        v_sc = [tile("v_sc%d" % a, [P, S], U8) for a in range(2)]
+        warm = tile("warm", [P, 2], F32)
+        tab_w = [tile("tab_w%d" % a, [P, T], U32, tag="slab%d" % a) for a in range(2)]
+        v_w = [[tile("v_w%d%d" % (a, c), [P, C], U32) for c in range(2)] for a in range(2)]
+        w2_raw = tile("w2_raw", [P, 2, 2 * M], U8)
+        w2_w = [tile("w2_w%d" % a, [P, 2 * M], U8) for a in range(2)]
+        w2_sc_raw = tile("w2_sc_raw", [P, 2, M], U8)
+        w2_sc = [tile("w2_sc%d" % a, [P, M], U8) for a in range(2)]
+        w1_w = [tile("w1_w%d" % a, [P, M], U32) for a in range(2)]
+        w1_sc = [tile("w1_sc%d" % a, [P, M], U8) for a in range(2)]
+        w3_w = [tile("w3_w0", [P, PASS], U32)]
+        w3_sc = [tile("w3_sc%d" % a, [P, PASS], U8) for a in range(2)]
+        w4_w = tile("w4_w", [P, 2, N], U32)
+        w4_sc = tile("w4_sc", [P, 2, N], U8)
         lift_sb = tile("lift_sb", [P, 4], F32)
         gain_sb = tile("gain_sb", [P, 2, 4], F32)
-        cap_sb = tile("cap_sb", [P, 3], F32)
-        wd = [tile("wd%d" % t, [P, S], F32) for t in range(4)]
-        sm = [tile("sm%d" % c, [P, 4, C], F32) for c in range(2)]
-        planes = [tile("planes%d" % i, [P, 4, C], BF16) for i in range(3)]
-        inter = [tile("inter%d" % i, [P, 4 * C], BF16) for i in range(3)]
-        tcode = [tile("tcode%d" % c, [P, C], U32) for c in range(2)]
-        tscale = [tile("tscale%d" % c, [P, C], U8) for c in range(2)]
-        hs = [tile("hs%d" % i, [P, S], F32) for i in range(2)]
-        xs = [tile("xs%d" % i, [P, PICKS], F32) for i in range(2)]
-        xc = {(1, c): tile("xc1%d" % c, [P, C], U32) for c in range(2)}
-        xsc = [[tile("xsc%d%d" % (a, c), [P, C], U8) for c in range(2)] for a in range(2)]
+        cap_sb = tile("cap_sb", [P, N_TILES], F32)
+        wgs_sb = [tile("wgs%d" % t, [P, S], F32) for t in range(4)]
+        wide = [tile("wide%d" % c, [P, 4, C], F32) for c in range(2)]
+        slices = [tile("slices%d" % i, [P, 4, C], BF16) for i in range(3)]
+        woven = [tile("woven%d" % i, [P, 4 * C], BF16) for i in range(3)]
+        top_w = [tile("top_w0", [P, C], U32)]
+        top_sc = [tile("top_sc%d" % c, [P, C], U8) for c in range(2)]
+        h_sb = [tile("h_sb%d" % i, [P, S], F32) for i in range(2)]
+        x_sb = [tile("x_sb%d" % i, [P, PICKS], F32) for i in range(2)]
+        x_w = {(1, c): tile("x_w1%d" % c, [P, C], U32) for c in range(2)}
+        x_sc = [[tile("x_sc%d%d" % (a, c), [P, C], U8) for c in range(2)] for a in range(2)]
 
-        nc.vector.memset(w2sr[:].rearrange("p a m -> p (a m)").bitcast(I32), 0)
-        nc.vector.memset(tsc[32:64, :].bitcast(I32), 0)
-        nc.vector.memset(tsc[64:128, :].bitcast(I32), 0)
-        nc.vector.memset(vs[0][:].bitcast(I32), 0)
-        nc.vector.memset(w4s[:].rearrange("p a m -> p (a m)").bitcast(I32), 0)
+        nc.vector.memset(w2_sc_raw[:].rearrange("p a m -> p (a m)").bitcast(I32), 0)
+        nc.vector.memset(tab_sc[32:64, :].bitcast(I32), 0)
+        nc.vector.memset(tab_sc[64:128, :].bitcast(I32), 0)
+        nc.vector.memset(v_sc[1][:].bitcast(I32), 0)
+        nc.gpsimd.memset(warm[:, 0:1], 0.0)
+        nc.scalar.activation(warm[:, 1:2], warm[:, 0:1], ACT.Silu)
+        nc.vector.memset(w4_sc[:].rearrange("p a m -> p (a m)").bitcast(I32), 0)
 
         def load_scale_rows(dst, src):
-            for q in range(4):
+            for g in range(4):
                 nc.sync.dma_start(
-                    out=dst[32 * q : 32 * q + 4].bitcast(I32),
-                    in_=src[:, 4 * q : 4 * q + 4, :].rearrange("a r n -> r a n").bitcast(I32),
+                    out=dst[32 * g : 32 * g + 4].bitcast(I32),
+                    in_=src[:, 4 * g : 4 * g + 4, :].rearrange("a r n -> r a n").bitcast(I32),
                 )
 
-        def load_raw(name, slot, rows):
-            raw = tile(name, [P, 4, 512], F32, tag="raw%d" % slot)
+        def load_weight(name, tag, rows):
+            raw = tile(name, [P, 4, PASS], F32, tag=tag)
             nc.sync.dma_start(out=raw[:], in_=rows.rearrange("(p j) c -> p j c", j=4))
             return raw
 
-        def load_tab(a):
+        def load_table(a):
             nc.sync.dma_start(
-                out=tabw[a][:].bitcast(I32), in_=tab_words[a].rearrange("p t i -> p (t i)").bitcast(I32)
+                out=tab_w[a][:].bitcast(I32), in_=tab_words[a].rearrange("p c i -> p (c i)").bitcast(I32)
             )
 
         pages = {}
 
-        def load_page(a, t):
-            i = 4 * a + t
-            pages[a, t] = tile("page%d" % i, [P, T2], F32, tag="page%d" % (i % 7))
+        def load_page(a, t, tag=None):
+            pages[a, t] = tile("page%d%d" % (a, t), [P, T2], F32, tag=tag)
             nc.sync.dma_start(out=pages[a, t][:], in_=page0.rearrange("(a p t) c -> a t p c", a=2, t=4)[a, t])
 
-        def load_wd(t):
+        def load_wgs(t):
             rows = wgs.rearrange("(i t) j -> t i j", t=4)[t]
             for g in range(4):
-                nc.sync.dma_start(out=wd[t][32 * g : 32 * g + 32, :], in_=rows)
+                nc.sync.dma_start(out=wgs_sb[t][32 * g : 32 * g + 32, :], in_=rows)
 
-        nc.sync.dma_start(o1[:], offs)
-        nc.sync.dma_start(out=tsc[0:32, :].bitcast(I32), in_=tab_scales.rearrange("a q t -> (a q) t").bitcast(I32))
-        nc.sync.dma_start(out=w2r[:].bitcast(I32), in_=w2_words.rearrange("a p w -> p a w").bitcast(I32))
-        load_scale_rows(w2sr, w2_scales)
-        load_tab(0)
-        w1r = [load_raw("w1r%d" % a, a, w1[512 * a : 512 * a + 512, :]) for a in range(2)]
-        load_tab(1)
+        nc.sync.dma_start(idx[:], offs)
+        nc.sync.dma_start(out=w2_raw[:].bitcast(I32), in_=w2_words.rearrange("a p w -> p a w").bitcast(I32))
+        nc.sync.dma_start(out=tab_sc[0:32, :].bitcast(I32), in_=tab_scales.rearrange("a s c -> (a s) c").bitcast(I32))
+        load_scale_rows(w2_sc_raw, w2_scales)
+        load_table(0)
+        w1_raw = [load_weight("w1_raw%d" % a, "raw%d" % a, w1[PASS * a : PASS * (a + 1), :]) for a in range(2)]
+        load_table(1)
         nc.sync.dma_start(out=lift_sb[:], in_=lift.rearrange("(p t) -> p t", t=4))
 
-        nc.vector.tensor_copy(gs[:], tsc[:].indirect(o1[:]))
-
-        def move_scale_rows(a):
-            for q in range(4):
-                nc.scalar.dma_start(
-                    out=vs[a][32 * q : 32 * q + 4, :].bitcast(I32),
-                    in_=gs[16 * a + 4 * q : 16 * a + 4 * q + 4, :].bitcast(I32),
-                )
-
-        move_scale_rows(0)
+        nc.vector.tensor_copy(picked_sc[:], tab_sc[:].indirect(idx[:]))
+        nc.vector.tensor_copy(v_sc[0][:].bitcast(I32), picked_sc[:].bitcast(I32))
+        moves = [(a, g) for a in range(2) for g in range(4)][1:]
+        for a, g in moves:
+            queue = nc.gpsimd if (a, g) == moves[-1] else nc.scalar
+            queue.dma_start(
+                out=v_sc[a][32 * g : 32 * g + 4, :].bitcast(I32),
+                in_=picked_sc[16 * a + 4 * g : 16 * a + 4 * g + 4, :].bitcast(I32),
+            )
         for a in range(2):
             nc.vector.tensor_copy(
-                w2d[a][:].rearrange("p (t q b) -> p q t b", t=4, b=2),
-                w2r[:, a, :].rearrange("p (q t b) -> p q t b", t=4, b=2),
+                w2_w[a][:].rearrange("p (t q b) -> p t q b", t=4, b=2),
+                w2_raw[:, a, :].rearrange("p (q t b) -> p t q b", t=4, b=2),
             )
             nc.vector.tensor_copy(
-                w2s[a][:].rearrange("p (t q) -> p q t", t=4), w2sr[:, a, :].rearrange("p (q t) -> p q t", t=4)
+                w2_sc[a][:].rearrange("p (t q) -> p t q", t=4),
+                w2_sc_raw[:, a, :].rearrange("p (q t) -> p t q", t=4),
             )
 
         def gather_words(a, c):
-            nc.vector.tensor_copy(vw[a][c][:], tabw[a][:].indirect(o1[:, LC * c : LC * c + LC]))
+            nc.vector.tensor_copy(v_w[a][c][:], tab_w[a][:].indirect(idx[:, LC * c : LC * c + LC]))
 
-        def cast_weight(raw, dst, copy=nc.scalar.copy, q=slice(0, 128)):
+        def cast_weight(copy, raw, dst, groups):
             copy(
-                dst[:].rearrange("p (t q j) -> p q j t", t=4, j=4)[:, q],
-                raw[:].rearrange("p j (q t) -> p q j t", t=4)[:, q],
+                dst[:].rearrange("p (t q j) -> p q j t", t=4, j=4)[:, groups],
+                raw[:].rearrange("p j (q t) -> p q j t", t=4)[:, groups],
             )
 
-        def quantize(src, codes, scales):
-            nc.vector.quantize_mx(out=codes[:].bitcast(FP8X4), scales=scales[:], in_=src[:])
+        def quantize(src, words, scales):
+            nc.vector.quantize_mx(out=words[:].bitcast(FP8X4), scales=scales[:], in_=src[:])
 
-        def interleave(copy, src, dst):
-            copy(
-                dst[:].rearrange("p (c i t) -> p c t i", i=4, t=4), src[:].rearrange("p t (c i) -> p c t i", i=4)
-            )
+        def weave(copy, src, dst):
+            copy(dst[:].rearrange("p (c i t) -> p c t i", i=4, t=4), src[:].rearrange("p t (c i) -> p c t i", i=4))
 
+        all_groups = slice(0, P)
         gather_words(0, 0)
         gather_words(0, 1)
-        cast_weight(w1r[0], inter[0])
-        vs.append(tile("vs1", [P, S], U8, tag="raw0"))
-        nc.vector.memset(vs[1][:].bitcast(I32), 0)
-        move_scale_rows(1)
-        quantize(inter[0], w1c[0], w1s[0])
-        cast_weight(w1r[1], inter[1])
-        quantize(inter[1], w1c[1], w1s[1])
+        for a, copy in enumerate((nc.vector.tensor_copy, nc.scalar.copy)):
+            cast_weight(copy, w1_raw[a], woven[a], all_groups)
+            quantize(woven[a], w1_w[a], w1_sc[a])
 
-        w3r0 = load_raw("w3r0", 2, w3[:, 0:512])
-        load_wd(0)
+        w3_raw = [load_weight("w3_raw0", "raw2", w3[:, 0:PASS])]
+        load_wgs(0)
         load_page(0, 0)
-        nc.sync.dma_start(o2[:], offs2)
-        load_wd(1)
+        nc.sync.dma_start(idx2[:], offs2)
+        load_wgs(1)
         load_page(0, 1)
-        w3r1 = load_raw("w3r1", 1, w3[:, 512:1024])
-        load_wd(2)
+        w3_raw.append(load_weight("w3_raw1", "raw0", w3[:, PASS : 2 * PASS]))
+        load_wgs(2)
         load_page(0, 2)
-        nc.sync.dma_start(o3[:], offs3)
         nc.sync.dma_start(out=gain_sb[:], in_=gain.rearrange("(a p t) -> p a t", a=2, t=4))
-        load_wd(3)
+        load_wgs(3)
         load_page(0, 3)
         for t in range(3):
             load_page(1, t)
-        nc.sync.dma_start(
-            out=w4c[:].bitcast(I32), in_=w4_words.rearrange("a p c i -> p a (c i)").bitcast(I32)
-        )
-        load_scale_rows(w4s, w4_scales)
-        nc.sync.dma_start(o4[:], offs4)
-        wgo_sb = tile("wgo_sb", [P, PICKS], F32, tag="tsc")
+        load_page(1, 3, tag="slab0")
+        nc.sync.dma_start(idx3[:], offs3)
+        nc.sync.dma_start(out=w4_w[:].bitcast(I32), in_=w4_words.rearrange("a p c i -> p a (c i)").bitcast(I32))
+        load_scale_rows(w4_sc, w4_scales)
+        nc.sync.dma_start(idx4[:], offs4)
+        wgo_sb = tile("wgo_sb", [P, PICKS], F32, tag="tab_sc")
         nc.sync.dma_start(out=wgo_sb[:], in_=wgo)
         with nc.allow_non_contiguous_dma(reason="one cap value for each partition and row tile"):
-            nc.sync.dma_start(out=cap_sb[:], in_=cap.rearrange("(c p) -> p c", p=P))
+            nc.sync.dma_start(out=cap_sb[:], in_=cap.rearrange("(n p) -> p n", p=P))
 
-        def stage1_pass(a, c, t):
-            cols = slice(128 * t, 128 * t + 128)
+        def first_products(a, c, t):
+            cols = slice(P * t, P * t + P)
             nc.tensor.matmul_mx(
-                out=banks[2 * t][:], lhsT=w1c[a][:, cols].bitcast(FP8X4), lhsT_scale=w1s[a][:, cols],
-                rhs=vw[a][c][:].bitcast(FP8X4), rhs_scale=vs[a][:, C * c : C * c + C], start=a == 0, stop=a == 1,
+                out=banks[2 * t][:], lhsT=w1_w[a][:, cols].bitcast(FP8X4), lhsT_scale=w1_sc[a][:, cols],
+                rhs=v_w[a][c][:].bitcast(FP8X4), rhs_scale=v_sc[a][:, C * c : C * c + C], start=a == 0, stop=a == 1,
             )
             nc.tensor.matmul_mx(
-                out=banks[2 * t + 1][:], lhsT=w2d[a][:, 256 * t : 256 * t + 256].bitcast(FP4X4),
-                lhsT_scale=w2s[a][:, cols],
-                rhs=vw[a][c][:].bitcast(FP8X4), rhs_scale=vs[a][:, C * c : C * c + C], start=a == 0, stop=a == 1,
+                out=banks[2 * t + 1][:], lhsT=w2_w[a][:, 2 * P * t : 2 * P * (t + 1)].bitcast(FP4X4),
+                lhsT_scale=w2_sc[a][:, cols],
+                rhs=v_w[a][c][:].bitcast(FP8X4), rhs_scale=v_sc[a][:, C * c : C * c + C], start=a == 0, stop=a == 1,
             )
 
         def silu(c, t):
-            nc.scalar.activation(sm[c][:, t, :], banks[2 * t][:], ACT.Silu)
+            nc.scalar.activation(wide[c][:, t, :], banks[2 * t][:], ACT.Silu)
 
         def larger(c, t):
-            nc.vector.tensor_tensor(sm[c][:, t, :], banks[2 * t + 1][:], sm[c][:, t, :], ALU.max)
+            nc.vector.tensor_tensor(wide[c][:, t, :], banks[2 * t + 1][:], wide[c][:, t, :], ALU.max)
 
         def lifted(c, t):
-            nc.scalar.activation(planes[c][:, t, :], sm[c][:, t, :], ACT.Copy, scale=lift_sb[:, t : t + 1])
+            nc.scalar.activation(slices[c][:, t, :], wide[c][:, t, :], ACT.Copy, scale=lift_sb[:, t : t + 1])
 
         for t in range(4):
-            stage1_pass(0, 0, t)
+            first_products(0, 0, t)
         gather_words(1, 0)
         gather_words(1, 1)
         for t in range(4):
-            stage1_pass(1, 0, t)
+            first_products(1, 0, t)
         for t in range(4):
             silu(0, t)
             larger(0, t)
             if t:
                 lifted(0, t - 1)
-            cast_weight(w3r0, inter[2], nc.vector.tensor_copy, slice(32 * t, 32 * t + 32))
-            stage1_pass(0, 1, t)
-            stage1_pass(1, 1, t)
+            cast_weight(nc.vector.tensor_copy, w3_raw[0], woven[2], slice(32 * t, 32 * t + 32))
+            for a in range(2):
+                first_products(a, 1, t)
         lifted(0, 3)
-        quantize(inter[2], w3c[0], w3s[0])
-        interleave(nc.vector.tensor_copy, planes[0], inter[0])
-        quantize(inter[0], tcode[0], tscale[0])
+        quantize(woven[2], w3_w[0], w3_sc[0])
+        weave(nc.vector.tensor_copy, slices[0], woven[0])
+        quantize(woven[0], top_w[0], top_sc[0])
         for t in range(4):
             silu(1, t)
 
-        steps = [(0, 0, [0]), (0, 1, [0]), (0, 2, [0]), (0, 0, [1]), (0, 1, [1]), (0, 2, [1]), (0, 3, [0, 1])]
-        steps.extend((1, t, [0, 1]) for t in range(4))
-
-        stages = [hs[i % 2][:] for i in range(len(steps))]
-        stages[2] = planes[1][:].rearrange("p t c -> p (t c)").bitcast(F32)
+        steps = [(0, t, [c]) for c in range(2) for t in range(3)]
+        steps.extend((i // 4, i % 4, [0, 1]) for i in range(3, 8))
+        staged = [h_sb[i % 2][:, C * chunks[0] : C * (chunks[-1] + 1)] for i, (a, t, chunks) in enumerate(steps)]
+        staged[1] = tile("h_step1", [P, C], F32, tag="top_w1")[:]
+        staged[2] = slices[1][:].rearrange("p t c -> p (t c)").bitcast(F32)[:, 0:C]
+        staged[4] = tile("h_step4", [P, C], F32, tag="w3_w1")[:]
 
         def states(i):
             a, t, chunks = steps[i]
+            cols = slice(P * t, P * t + P)
             for c in chunks:
                 bank = banks[i % 2 * 2 + c]
                 nc.tensor.matmul_mx(
-                    out=bank[:], lhsT=w3c[a][:, 128 * t : 128 * t + 128].bitcast(FP8X4),
-                    lhsT_scale=w3s[a][:, 128 * t : 128 * t + 128],
-                    rhs=tcode[c][:].bitcast(FP8X4), rhs_scale=tscale[c][:], start=True, stop=True,
+                    out=bank[:], lhsT=w3_w[a][:, cols].bitcast(FP8X4), lhsT_scale=w3_sc[a][:, cols],
+                    rhs=top_w[c][:].bitcast(FP8X4), rhs_scale=top_sc[c][:], start=True, stop=True,
                 )
-                nc.scalar.copy(stages[i][:, C * c : C * c + C], bank[:])
+                nc.scalar.copy(staged[i][:, C * (c - chunks[0]) : C * (c - chunks[0] + 1)], bank[:])
 
         def put(i):
             a, t, chunks = steps[i]
             lo, hi = chunks[0], chunks[-1] + 1
             nc.vector.tensor_tensor(
-                pages[a, t][:].indirect(o2[:, LC * lo : LC * hi]), stages[i][:, C * lo : C * hi],
-                wd[t][:, C * lo : C * hi], ALU.mult,
+                pages[a, t][:].indirect(idx2[:, LC * lo : LC * hi]), staged[i], wgs_sb[t][:, C * lo : C * hi], ALU.mult
             )
-
-        def fetch(a, t, chunks, dst, x_planes):
-            lo, hi = chunks[0], chunks[-1] + 1
-            nc.vector.tensor_copy(dst, pages[a, t][:].indirect(o3[:, LC * lo : LC * hi]))
-            for c in chunks:
-                nc.scalar.activation(
-                    x_planes[c][:, t, :], dst[:, C * (c - lo) : C * (c - lo + 1)], ACT.Copy,
-                    scale=gain_sb[:, a, t : t + 1],
-                )
 
         states(0)
         states(1)
@@ -264,92 +252,90 @@ def tile_list_call_triage_page_kernel(
             larger(1, t)
             lifted(1, t)
         put(1)
-        interleave(nc.scalar.copy, planes[1], inter[1])
+        weave(nc.scalar.copy, slices[1], woven[1])
         states(2)
-        quantize(inter[1], tcode[1], tscale[1])
-        cast_weight(w3r1, inter[2])
+        top_w.append(tile("top_w1", [P, C], U32))
+        quantize(woven[1], top_w[1], top_sc[1])
+        cast_weight(nc.scalar.copy, w3_raw[1], woven[2], all_groups)
         states(3)
         put(2)
-        quantize(inter[2], w3c[1], w3s[1])
         states(4)
         put(3)
         states(5)
         put(4)
+        w3_w.append(tile("w3_w1", [P, PASS], U32))
+        quantize(woven[2], w3_w[1], w3_sc[1])
         states(6)
-        xp0 = [planes[2], planes[0]]
-        xp1 = [planes[1], planes[2]]
-        fetch(0, 0, [0, 1], xs[0][:], xp0)
-        load_page(1, 3)
-        outs = [
-            tile("out0", [P, T2], F32, tag="slab0"),
-            tile("out1", [P, T2], F32, tag="slab1"),
-            tile("out2", [P, T2], F32, tag="raw2"),
-        ]
-        for n in range(3):
+        outs = [tile("out%d" % n, [P, T2], F32, tag=tag) for n, tag in enumerate(("slab1", "raw1", "raw2"))]
+        for n in range(N_TILES):
             nc.sync.dma_start(out=outs[n][:], in_=page1[P * n : P * n + P, :])
-        put(5)
-        states(7)
-        fetch(0, 1, [0, 1], xs[1][:], xp0)
-        put(6)
-        states(8)
-        fetch(0, 2, [0, 1], xs[0][:], xp0)
-        put(7)
-        states(9)
-        fetch(0, 3, [0, 1], xs[1][:], xp0)
-        put(8)
-        states(10)
-        halves = [xs[i // 2][:, C * (i % 2) : C * (i % 2) + C] for i in range(4)]
-        fetch(1, 0, [0], halves[0], xp1)
-        interleave(nc.scalar.copy, xp0[0], inter[0])
-        xc[0, 0] = tile("xc00", [P, C], U32, tag="wd1")
-        quantize(inter[0], xc[0, 0], xsc[0][0])
-        put(9)
-        fetch(1, 1, [0], halves[1], xp1)
-        interleave(nc.scalar.copy, xp0[1], inter[1])
-        xc[0, 1] = tile("xc01", [P, C], U32, tag="wd2")
-        quantize(inter[1], xc[0, 1], xsc[0][1])
-        put(10)
-        fetch(1, 2, [0], halves[2], xp1)
-        fetch(1, 3, [0], halves[3], xp1)
-        interleave(nc.scalar.copy, xp1[0], inter[2])
-        fetch(1, 3, [1], halves[0], xp1)
-        fetch(1, 2, [1], hs[0][:, 0:C], xp1)
-        fetch(1, 0, [1], hs[0][:, C : 2 * C], xp1)
+        for i in range(5, len(steps)):
+            put(i)
+            if i + 2 < len(steps):
+                states(i + 2)
+
+        def fetch(a, t, chunks, dst):
+            lo, hi = chunks[0], chunks[-1] + 1
+            nc.vector.tensor_copy(dst, pages[a, t][:].indirect(idx3[:, LC * lo : LC * hi]))
+            for c in chunks:
+                nc.scalar.activation(
+                    x_slices[a][c][:, t, :], dst[:, C * (c - lo) : C * (c - lo + 1)], ACT.Copy,
+                    scale=gain_sb[:, a, t : t + 1],
+                )
+
+        x_slices = [[slices[2], slices[0]], [slices[1], slices[2]]]
+        x_woven = [[woven[0], woven[1]], [woven[2], woven[0]]]
+        picked = [x_sb[0], x_sb[1], h_sb[1], h_sb[0]]
+        halves = [picked[i // 2][:, C * (i % 2) : C * (i % 2) + C] for i in range(8)]
+        for t in range(4):
+            fetch(0, t, [0, 1], picked[t][:])
+        weave(nc.scalar.copy, x_slices[0][0], x_woven[0][0])
+        for t in range(4):
+            fetch(1, t, [0], halves[t])
+        x_w[0, 0] = tile("x_w00", [P, C], U32, tag="wgs1")
+        quantize(x_woven[0][0], x_w[0, 0], x_sc[0][0])
+        weave(nc.scalar.copy, x_slices[1][0], x_woven[1][0])
+        weave(nc.scalar.copy, x_slices[0][1], x_woven[0][1])
+        for t in range(3):
+            fetch(1, t, [1], halves[4 + t])
+
+        def score_bank(c, n):
+            return banks[4 * (1 - c) + n]
 
         def scores(c):
-            quantize(inter[2 - 2 * c], xc[1, c], xsc[1][c])
-            for n in range(3):
-                bank = banks[4 + n if c == 0 else n]
+            quantize(x_woven[1][c], x_w[1, c], x_sc[1][c])
+            for n in range(N_TILES):
                 cols = slice(P * n, P * n + P)
                 for a in range(2):
                     nc.tensor.matmul_mx(
-                        out=bank[:], lhsT=w4c[:, a, cols].bitcast(FP8X4), lhsT_scale=w4s[:, a, cols],
-                        rhs=xc[a, c][:].bitcast(FP8X4), rhs_scale=xsc[a][c][:], start=a == 0, stop=a == 1,
+                        out=score_bank(c, n)[:], lhsT=w4_w[:, a, cols].bitcast(FP8X4), lhsT_scale=w4_sc[:, a, cols],
+                        rhs=x_w[a, c][:].bitcast(FP8X4), rhs_scale=x_sc[a][c][:], start=a == 0, stop=a == 1,
                     )
 
         def capped(c, n, dst):
             nc.vector.scalar_tensor_tensor(
-                dst, banks[4 + n if c == 0 else n][:], cap_sb[:, n : n + 1], wgo_sb[:, C * c : C * c + C],
-                ALU.min, ALU.mult,
+                dst, score_bank(c, n)[:], cap_sb[:, n : n + 1], wgo_sb[:, C * c : C * c + C], ALU.min, ALU.mult
             )
 
         def place(c, n, src):
-            nc.vector.tensor_copy(outs[n][:].indirect(o4[:, LC * c : LC * c + LC]), src)
+            nc.vector.tensor_copy(outs[n][:].indirect(idx4[:, LC * c : LC * c + LC]), src)
 
         scores(0)
-        last_x = tile("last_x", [P, C], F32, tag="inter2")
-        fetch(1, 1, [1], last_x[:], xp1)
-        interleave(nc.scalar.copy, xp1[1], inter[0])
-        capped(0, 0, sm[0][:, 0, :])
-        capped(0, 1, sm[0][:, 1, :])
-        place(0, 0, sm[0][:, 0, :])
-        place(0, 1, sm[0][:, 1, :])
+        last_x = tile("last_x", [P, C], F32, tag="woven2")
+        fetch(1, 3, [1], last_x[:])
+        weave(nc.scalar.copy, x_slices[1][1], x_woven[1][1])
+        for n in range(N_TILES - 1):
+            capped(0, n, wide[0][:, n, :])
+        for n in range(N_TILES - 1):
+            place(0, n, wide[0][:, n, :])
+        x_w[0, 1] = tile("x_w01", [P, C], U32, tag="wgs2")
+        quantize(x_woven[0][1], x_w[0, 1], x_sc[0][1])
         scores(1)
-        late_y = tile("late_y", [P, C], F32, tag="inter0")
-        capped(0, 2, late_y[:])
-        place(0, 2, late_y[:])
-        for n in range(3):
-            capped(1, n, sm[1][:, n, :])
-        for n in range(3):
-            place(1, n, sm[1][:, n, :])
+        last_y = tile("last_y", [P, C], F32, tag="woven0")
+        capped(0, N_TILES - 1, last_y[:])
+        place(0, N_TILES - 1, last_y[:])
+        for n in range(N_TILES):
+            capped(1, n, wide[1][:, n, :])
+        for n in range(N_TILES):
+            place(1, n, wide[1][:, n, :])
             nc.sync.dma_start(out=out[P * n : P * n + P, :], in_=outs[n][:])

from contextlib import ExitStack

import concourse.mybir as mybir

K, T, S, PICKS, T2, M, H, N = 1024, 4096, 1024, 1024, 2048, 512, 1024, 384
FLOPS = 2 * (2 * K * M * S + M * H * S + H * N * PICKS)

F32 = mybir.dt.float32
BF16 = mybir.dt.bfloat16
I32 = mybir.dt.int32
U32 = mybir.dt.uint32
U16 = mybir.dt.uint16
U8 = mybir.dt.uint8
FP8X4 = mybir.dt.float8_e4m3fn_x4
FP4X4 = mybir.dt.float4_e2m1fn_x4
ALU = mybir.AluOpType
ACT = mybir.ActivationFunctionType

P = 128
PASS = 512
C = 512
LC = C // 16
N_TILES = N // P


def tile_list_call_triage_page_kernel(
    tc, tab_words, tab_scales, offs, offs2, offs3, offs4, w1, w2_words, w2_scales, lift, w3, wgs, page0, gain,
    w4_words, w4_scales, cap, wgo, page1, out,
):
    nc = tc.nc
    with ExitStack() as ctx:
        sb = ctx.enter_context(tc.tile_pool(name="sb", bufs=1))
        ps = ctx.enter_context(tc.psum_pool(name="ps", bufs=1))

        def tile(name, shape, dtype, tag=None):
            return sb.tile(shape, dtype, name=name, tag=tag or name, align_bytes=64)

        banks = [ps.tile([P, C], F32, name="bank%d" % i) for i in range(8)]

        idx, idx2, idx3, idx4 = [tile("list%d" % i, [P, S // 16], U16) for i in range(4)]
        tab_sc = tile("tab_sc", [P, T], U8)
        picked_sc = tile("picked_sc", [P, S], U8)
        v_sc = [tile("v_sc%d" % a, [P, S], U8) for a in range(2)]
        warm = tile("warm", [P, 2], F32)
        tab_w = [tile("tab_w%d" % a, [P, T], U32, tag="slab%d" % a) for a in range(2)]
        v_w = [[tile("v_w%d%d" % (a, c), [P, C], U32) for c in range(2)] for a in range(2)]
        w2_raw = tile("w2_raw", [P, 2, 2 * M], U8)
        w2_w = [tile("w2_w%d" % a, [P, 2 * M], U8) for a in range(2)]
        w2_sc_raw = tile("w2_sc_raw", [P, 2, M], U8)
        w2_sc = [tile("w2_sc%d" % a, [P, M], U8) for a in range(2)]
        w1_w = [tile("w1_w%d" % a, [P, M], U32) for a in range(2)]
        w1_sc = [tile("w1_sc%d" % a, [P, M], U8) for a in range(2)]
        w3_w = [tile("w3_w0", [P, PASS], U32)]
        w3_sc = [tile("w3_sc%d" % a, [P, PASS], U8) for a in range(2)]
        w4_w = tile("w4_w", [P, 2, N], U32)
        w4_sc = tile("w4_sc", [P, 2, N], U8)
        lift_sb = tile("lift_sb", [P, 4], F32)
        gain_sb = tile("gain_sb", [P, 2, 4], F32)
        cap_sb = tile("cap_sb", [P, N_TILES], F32)
        wgs_sb = [tile("wgs%d" % t, [P, S], F32) for t in range(4)]
        wide = [tile("wide%d" % c, [P, 4, C], F32) for c in range(2)]
        slices = [tile("slices%d" % i, [P, 4, C], BF16) for i in range(3)]
        woven = [tile("woven%d" % i, [P, 4 * C], BF16) for i in range(3)]
        top_w = [tile("top_w0", [P, C], U32)]
        top_sc = [tile("top_sc%d" % c, [P, C], U8) for c in range(2)]
        h_sb = [tile("h_sb%d" % i, [P, S], F32) for i in range(2)]
        x_sb = [tile("x_sb%d" % i, [P, PICKS], F32) for i in range(2)]
        x_w = {(1, c): tile("x_w1%d" % c, [P, C], U32) for c in range(2)}
        x_sc = [[tile("x_sc%d%d" % (a, c), [P, C], U8) for c in range(2)] for a in range(2)]

        nc.vector.memset(w2_sc_raw[:].rearrange("p a m -> p (a m)").bitcast(I32), 0)
        nc.vector.memset(tab_sc[32:64, :].bitcast(I32), 0)
        nc.vector.memset(tab_sc[64:128, :].bitcast(I32), 0)
        nc.vector.memset(v_sc[1][:].bitcast(I32), 0)
        nc.gpsimd.memset(warm[:, 0:1], 0.0)
        nc.scalar.activation(warm[:, 1:2], warm[:, 0:1], ACT.Silu)
        nc.vector.memset(w4_sc[:].rearrange("p a m -> p (a m)").bitcast(I32), 0)

        def load_scale_rows(dst, src):
            for g in range(4):
                nc.sync.dma_start(
                    out=dst[32 * g : 32 * g + 4].bitcast(I32),
                    in_=src[:, 4 * g : 4 * g + 4, :].rearrange("a r n -> r a n").bitcast(I32),
                )

        def load_weight(name, tag, rows):
            raw = tile(name, [P, 4, PASS], F32, tag=tag)
            nc.sync.dma_start(out=raw[:], in_=rows.rearrange("(p j) c -> p j c", j=4))
            return raw

        def load_table(a):
            nc.sync.dma_start(
                out=tab_w[a][:].bitcast(I32), in_=tab_words[a].rearrange("p c i -> p (c i)").bitcast(I32)
            )

        pages = {}

        def load_page(a, t, tag=None):
            pages[a, t] = tile("page%d%d" % (a, t), [P, T2], F32, tag=tag)
            nc.sync.dma_start(out=pages[a, t][:], in_=page0.rearrange("(a p t) c -> a t p c", a=2, t=4)[a, t])

        def load_wgs(t):
            rows = wgs.rearrange("(i t) j -> t i j", t=4)[t]
            for g in range(4):
                nc.sync.dma_start(out=wgs_sb[t][32 * g : 32 * g + 32, :], in_=rows)

        nc.sync.dma_start(idx[:], offs)
        nc.sync.dma_start(out=w2_raw[:].bitcast(I32), in_=w2_words.rearrange("a p w -> p a w").bitcast(I32))
        nc.sync.dma_start(out=tab_sc[0:32, :].bitcast(I32), in_=tab_scales.rearrange("a s c -> (a s) c").bitcast(I32))
        load_scale_rows(w2_sc_raw, w2_scales)
        load_table(0)
        w1_raw = [load_weight("w1_raw%d" % a, "raw%d" % a, w1[PASS * a : PASS * (a + 1), :]) for a in range(2)]
        load_table(1)
        nc.sync.dma_start(out=lift_sb[:], in_=lift.rearrange("(p t) -> p t", t=4))

        nc.vector.tensor_copy(picked_sc[:], tab_sc[:].indirect(idx[:]))
        nc.vector.tensor_copy(v_sc[0][:].bitcast(I32), picked_sc[:].bitcast(I32))
        moves = [(a, g) for a in range(2) for g in range(4)][1:]
        for a, g in moves:
            queue = nc.gpsimd if (a, g) == moves[-1] else nc.scalar
            queue.dma_start(
                out=v_sc[a][32 * g : 32 * g + 4, :].bitcast(I32),
                in_=picked_sc[16 * a + 4 * g : 16 * a + 4 * g + 4, :].bitcast(I32),
            )
        for a in range(2):
            nc.vector.tensor_copy(
                w2_w[a][:].rearrange("p (t q b) -> p t q b", t=4, b=2),
                w2_raw[:, a, :].rearrange("p (q t b) -> p t q b", t=4, b=2),
            )
            nc.vector.tensor_copy(
                w2_sc[a][:].rearrange("p (t q) -> p t q", t=4),
                w2_sc_raw[:, a, :].rearrange("p (q t) -> p t q", t=4),
            )

        def gather_words(a, c):
            nc.vector.tensor_copy(v_w[a][c][:], tab_w[a][:].indirect(idx[:, LC * c : LC * c + LC]))

        def cast_weight(copy, raw, dst, groups):
            copy(
                dst[:].rearrange("p (t q j) -> p q j t", t=4, j=4)[:, groups],
                raw[:].rearrange("p j (q t) -> p q j t", t=4)[:, groups],
            )

        def quantize(src, words, scales):
            nc.vector.quantize_mx(out=words[:].bitcast(FP8X4), scales=scales[:], in_=src[:])

        def weave(copy, src, dst):
            copy(dst[:].rearrange("p (c i t) -> p c t i", i=4, t=4), src[:].rearrange("p t (c i) -> p c t i", i=4))

        all_groups = slice(0, P)
        gather_words(0, 0)
        gather_words(0, 1)
        for a, copy in enumerate((nc.vector.tensor_copy, nc.scalar.copy)):
            cast_weight(copy, w1_raw[a], woven[a], all_groups)
            quantize(woven[a], w1_w[a], w1_sc[a])

        w3_raw = [load_weight("w3_raw0", "raw2", w3[:, 0:PASS])]
        load_wgs(0)
        load_page(0, 0)
        nc.sync.dma_start(idx2[:], offs2)
        load_wgs(1)
        load_page(0, 1)
        w3_raw.append(load_weight("w3_raw1", "raw0", w3[:, PASS : 2 * PASS]))
        load_wgs(2)
        load_page(0, 2)
        nc.sync.dma_start(out=gain_sb[:], in_=gain.rearrange("(a p t) -> p a t", a=2, t=4))
        load_wgs(3)
        load_page(0, 3)
        for t in range(3):
            load_page(1, t)
        load_page(1, 3, tag="slab0")
        nc.sync.dma_start(idx3[:], offs3)
        nc.sync.dma_start(out=w4_w[:].bitcast(I32), in_=w4_words.rearrange("a p c i -> p a (c i)").bitcast(I32))
        load_scale_rows(w4_sc, w4_scales)
        nc.sync.dma_start(idx4[:], offs4)
        wgo_sb = tile("wgo_sb", [P, PICKS], F32, tag="tab_sc")
        nc.sync.dma_start(out=wgo_sb[:], in_=wgo)
        with nc.allow_non_contiguous_dma(reason="one cap value for each partition and row tile"):
            nc.sync.dma_start(out=cap_sb[:], in_=cap.rearrange("(n p) -> p n", p=P))

        def first_products(a, c, t):
            cols = slice(P * t, P * t + P)
            nc.tensor.matmul_mx(
                out=banks[2 * t][:], lhsT=w1_w[a][:, cols].bitcast(FP8X4), lhsT_scale=w1_sc[a][:, cols],
                rhs=v_w[a][c][:].bitcast(FP8X4), rhs_scale=v_sc[a][:, C * c : C * c + C], start=a == 0, stop=a == 1,
            )
            nc.tensor.matmul_mx(
                out=banks[2 * t + 1][:], lhsT=w2_w[a][:, 2 * P * t : 2 * P * (t + 1)].bitcast(FP4X4),
                lhsT_scale=w2_sc[a][:, cols],
                rhs=v_w[a][c][:].bitcast(FP8X4), rhs_scale=v_sc[a][:, C * c : C * c + C], start=a == 0, stop=a == 1,
            )

        def silu(c, t):
            nc.scalar.activation(wide[c][:, t, :], banks[2 * t][:], ACT.Silu)

        def larger(c, t):
            nc.vector.tensor_tensor(wide[c][:, t, :], banks[2 * t + 1][:], wide[c][:, t, :], ALU.max)

        def lifted(c, t):
            nc.scalar.activation(slices[c][:, t, :], wide[c][:, t, :], ACT.Copy, scale=lift_sb[:, t : t + 1])

        for t in range(4):
            first_products(0, 0, t)
        gather_words(1, 0)
        gather_words(1, 1)
        for t in range(4):
            first_products(1, 0, t)
        for t in range(4):
            silu(0, t)
            larger(0, t)
            if t:
                lifted(0, t - 1)
            cast_weight(nc.vector.tensor_copy, w3_raw[0], woven[2], slice(32 * t, 32 * t + 32))
            for a in range(2):
                first_products(a, 1, t)
        lifted(0, 3)
        quantize(woven[2], w3_w[0], w3_sc[0])
        weave(nc.vector.tensor_copy, slices[0], woven[0])
        quantize(woven[0], top_w[0], top_sc[0])
        for t in range(4):
            silu(1, t)

        steps = [(0, t, [c]) for c in range(2) for t in range(3)]
        steps.extend((i // 4, i % 4, [0, 1]) for i in range(3, 8))
        staged = [h_sb[i % 2][:, C * chunks[0] : C * (chunks[-1] + 1)] for i, (a, t, chunks) in enumerate(steps)]
        staged[1] = tile("h_step1", [P, C], F32, tag="top_w1")[:]
        staged[2] = slices[1][:].rearrange("p t c -> p (t c)").bitcast(F32)[:, 0:C]
        staged[4] = tile("h_step4", [P, C], F32, tag="w3_w1")[:]

        def states(i):
            a, t, chunks = steps[i]
            cols = slice(P * t, P * t + P)
            for c in chunks:
                bank = banks[i % 2 * 2 + c]
                nc.tensor.matmul_mx(
                    out=bank[:], lhsT=w3_w[a][:, cols].bitcast(FP8X4), lhsT_scale=w3_sc[a][:, cols],
                    rhs=top_w[c][:].bitcast(FP8X4), rhs_scale=top_sc[c][:], start=True, stop=True,
                )
                nc.scalar.copy(staged[i][:, C * (c - chunks[0]) : C * (c - chunks[0] + 1)], bank[:])

        def put(i):
            a, t, chunks = steps[i]
            lo, hi = chunks[0], chunks[-1] + 1
            nc.vector.tensor_tensor(
                pages[a, t][:].indirect(idx2[:, LC * lo : LC * hi]), staged[i], wgs_sb[t][:, C * lo : C * hi], ALU.mult
            )

        states(0)
        states(1)
        put(0)
        for t in range(4):
            larger(1, t)
            lifted(1, t)
        put(1)
        weave(nc.scalar.copy, slices[1], woven[1])
        states(2)
        top_w.append(tile("top_w1", [P, C], U32))
        quantize(woven[1], top_w[1], top_sc[1])
        cast_weight(nc.scalar.copy, w3_raw[1], woven[2], all_groups)
        states(3)
        put(2)
        states(4)
        put(3)
        states(5)
        put(4)
        w3_w.append(tile("w3_w1", [P, PASS], U32))
        quantize(woven[2], w3_w[1], w3_sc[1])
        states(6)
        outs = [tile("out%d" % n, [P, T2], F32, tag=tag) for n, tag in enumerate(("slab1", "raw1", "raw2"))]
        for n in range(N_TILES):
            nc.sync.dma_start(out=outs[n][:], in_=page1[P * n : P * n + P, :])
        for i in range(5, len(steps)):
            put(i)
            if i + 2 < len(steps):
                states(i + 2)

        def fetch(a, t, chunks, dst):
            lo, hi = chunks[0], chunks[-1] + 1
            nc.vector.tensor_copy(dst, pages[a, t][:].indirect(idx3[:, LC * lo : LC * hi]))
            for c in chunks:
                nc.scalar.activation(
                    x_slices[a][c][:, t, :], dst[:, C * (c - lo) : C * (c - lo + 1)], ACT.Copy,
                    scale=gain_sb[:, a, t : t + 1],
                )

        x_slices = [[slices[2], slices[0]], [slices[1], slices[2]]]
        x_woven = [[woven[0], woven[1]], [woven[2], woven[0]]]
        picked = [x_sb[0], x_sb[1], h_sb[1], h_sb[0]]
        halves = [picked[i // 2][:, C * (i % 2) : C * (i % 2) + C] for i in range(8)]
        for t in range(4):
            fetch(0, t, [0, 1], picked[t][:])
        weave(nc.scalar.copy, x_slices[0][0], x_woven[0][0])
        for t in range(4):
            fetch(1, t, [0], halves[t])
        x_w[0, 0] = tile("x_w00", [P, C], U32, tag="wgs1")
        quantize(x_woven[0][0], x_w[0, 0], x_sc[0][0])
        weave(nc.scalar.copy, x_slices[1][0], x_woven[1][0])
        weave(nc.scalar.copy, x_slices[0][1], x_woven[0][1])
        for t in range(3):
            fetch(1, t, [1], halves[4 + t])

        def score_bank(c, n):
            return banks[4 * (1 - c) + n]

        def scores(c):
            quantize(x_woven[1][c], x_w[1, c], x_sc[1][c])
            for n in range(N_TILES):
                cols = slice(P * n, P * n + P)
                for a in range(2):
                    nc.tensor.matmul_mx(
                        out=score_bank(c, n)[:], lhsT=w4_w[:, a, cols].bitcast(FP8X4), lhsT_scale=w4_sc[:, a, cols],
                        rhs=x_w[a, c][:].bitcast(FP8X4), rhs_scale=x_sc[a][c][:], start=a == 0, stop=a == 1,
                    )

        def capped(c, n, dst):
            nc.vector.scalar_tensor_tensor(
                dst, score_bank(c, n)[:], cap_sb[:, n : n + 1], wgo_sb[:, C * c : C * c + C], ALU.min, ALU.mult
            )

        def place(c, n, src):
            nc.vector.tensor_copy(outs[n][:].indirect(idx4[:, LC * c : LC * c + LC]), src)

        scores(0)
        last_x = tile("last_x", [P, C], F32, tag="woven2")
        fetch(1, 3, [1], last_x[:])
        weave(nc.scalar.copy, x_slices[1][1], x_woven[1][1])
        for n in range(N_TILES - 1):
            capped(0, n, wide[0][:, n, :])
        for n in range(N_TILES - 1):
            place(0, n, wide[0][:, n, :])
        x_w[0, 1] = tile("x_w01", [P, C], U32, tag="wgs2")
        quantize(x_woven[0][1], x_w[0, 1], x_sc[0][1])
        scores(1)
        last_y = tile("last_y", [P, C], F32, tag="woven0")
        capped(0, N_TILES - 1, last_y[:])
        place(0, N_TILES - 1, last_y[:])
        for n in range(N_TILES):
            capped(1, n, wide[1][:, n, :])
        for n in range(N_TILES):
            place(1, n, wide[1][:, n, :])
            nc.sync.dma_start(out=out[P * n : P * n + P, :], in_=outs[n][:])
